import numpy as np
import ml_dtypes


def mxq(x, axis, fmt="e4m3"):
    dtype, down = {"e4m3": (ml_dtypes.float8_e4m3fn, 7), "e5m2": (ml_dtypes.float8_e5m2, 14)}[fmt]
    v = np.moveaxis(np.asarray(x, np.float32).astype(ml_dtypes.bfloat16).astype(np.float64), axis, -1)
    blocks = v.reshape(v.shape[:-1] + (-1, 32))
    amax = np.abs(blocks).max(-1, keepdims=True)
    byte = np.maximum(np.where(amax > 0, np.frexp(amax)[1] - 1 + 127, 0) - down, 1)
    scale = np.exp2(byte - 127.0)
    codes = (blocks / scale).astype(np.float32).astype(dtype).astype(np.float64)
    return np.moveaxis((codes * scale).reshape(v.shape), -1, axis)


WIDE = False


def mx_kscale(k):
    if not WIDE:
        return np.ones(k)
    levels = np.array([10, -10, 5, -5, 0])
    if k % 512:
        return np.exp2(np.random.permutation(np.resize(levels, k // 32))).repeat(32)
    a = np.empty((k // 512, 16))
    for p in range(k // 512):
        a[p, :8] = np.random.permutation(np.resize(levels, 8))
        for g in range(8):
            far = levels[np.abs(levels - a[p, g]) >= 10]
            a[p, g + 8] = far[np.random.randint(len(far))]
    return np.exp2(a.ravel()).repeat(32)


def f64(x):
    return np.asarray(x).astype(np.float64)


def striped(idx):
    return np.tile(idx.reshape(-1, 16).T, (8, 1)).astype(np.uint16)


def unstriped(offs):
    return offs[:16].T.reshape(-1).astype(np.int64)


def striped8(idx):
    return np.concatenate([x.reshape(-1, 16).T for x in idx]).astype(np.uint16)


def runs(offs, k):
    lists = np.stack([offs[16 * r : 16 * r + 16].T.reshape(-1) for r in range(8)]).astype(np.int64)
    return lists[np.arange(k) % 512 // 64]


def pack_weight(w):
    k, n = w.shape
    w = f64(np.asarray(w, np.float32).astype(ml_dtypes.bfloat16)).reshape(k // 32, 32, n)
    amax = np.abs(w).max(1)
    byte = np.clip(np.where(amax > 0, np.frexp(amax)[1] - 1 + 127 - 7, 1), 1, 254)
    scaled = (w * np.exp2(127.0 - byte)[:, None, :]).reshape(k, n).astype(np.float32)
    words = np.ascontiguousarray(scaled.reshape(k // 512, 128, 4, n).transpose(0, 1, 3, 2)).astype(ml_dtypes.float8_e4m3fn).view(np.uint8)
    return words, np.ascontiguousarray(byte.astype(np.uint8).reshape(k // 512, 16, n))


def unpack_weight(words, scales):
    g, p, n, _ = words.shape
    vals = np.ascontiguousarray(words).view(ml_dtypes.float8_e4m3fn).astype(np.float64) * np.repeat(np.exp2(scales.astype(np.float64) - 127.0), 8, axis=1)[..., None]
    return vals.transpose(0, 1, 3, 2).reshape(g * 512, n)


K, T, S, N, G, H, W, U = 512, 2048, 256, 512, 2048, 512, 128, 512


def setup_inputs():
    n = np.random.standard_normal
    s = mx_kscale(K)[:, None]
    u = mx_kscale(K)
    packed_xT = pack_weight(n((K, T)) * s)
    packed_dT = pack_weight(n((K, G)) / s)
    perm = np.random.permutation(S)
    perm2 = np.random.permutation(U)
    return {
        "x_words": packed_xT[0],
        "x_scales": packed_xT[1],
        "d_words": packed_dT[0],
        "d_scales": packed_dT[1],
        "gn": (np.random.uniform(0.5, 1.5, (H, 1)) * u[:, None]).astype(np.float32),
        "w1": (n((H, N)) / np.sqrt(H) / u[:, None]).astype(np.float32),
        "offs": striped(np.random.permutation(T)[:S]),
        "k1": striped8(np.random.randint(0, G, (8, H))),
        "n1": striped(perm[:W]),
        "n2": striped(perm[W:]),
        "n3": striped(np.random.permutation(S)),
        "n4": striped(perm2[:S]),
        "n5": striped(perm2[S:]),
        "n6": striped(np.random.permutation(S)),
    }


def reference(x_words, x_scales, d_words, d_scales, gn, w1, offs, k1, n1, n2, n3, n4, n5, n6):
    d_k1 = unpack_weight(d_words, d_scales)[np.arange(K)[:, None], runs(k1, K)]
    xq = unpack_weight(x_words, x_scales)[:, unstriped(offs)]
    h = 0.0625 * (d_k1.T @ xq)
    pa = h[:, unstriped(n1)]
    pb = h[:, unstriped(n2)]
    rb = pa - pb
    ds = np.zeros((H, S))
    ds[:, unstriped(n1)] = pb
    dt = ds.copy()
    dt[:, unstriped(n2)] = rb
    z = f64(gn) * (np.maximum(dt, 0.5 * dt[:, unstriped(n3)]))
    h2 = mxq(f64(w1), 0, "e4m3").T @ mxq(z, 0, "e4m3")
    nw = h2 - h2[:, unstriped(n6)]
    ph = np.zeros((N, U))
    ph[:, unstriped(n4)] = h2
    out = ph.copy()
    out[:, unstriped(n5)] = nw
    return out

@@ -1,0 +1,183 @@
+from contextlib import ExitStack
+
+import concourse.mybir as mybir
+
+K, T, S, N, G, H, W, U = 512, 2048, 256, 512, 2048, 512, 128, 512
+FLOPS = 2 * K * H * S + 2 * H * N * S
+
+F32 = mybir.dt.float32
+BF16 = mybir.dt.bfloat16
+I32 = mybir.dt.int32
+U32 = mybir.dt.uint32
+U16 = mybir.dt.uint16
+U8 = mybir.dt.uint8
+FP8X4 = mybir.dt.float8_e4m3fn_x4
+ALU = mybir.AluOpType
+COPY = mybir.ActivationFunctionType.Copy
+
+P = 128
+PACK = 4
+HALF = S // 2
+LIST_ROWS = 16
+
+
+def tile_picked_pqlayswapdpagq_none_p_kernel(tc, x_words, x_scales, d_words, d_scales, gn, w1, offs, k1, n1, n2, n3, n4, n5, n6, out):
+    nc = tc.nc
+    with ExitStack() as ctx:
+        lists = ctx.enter_context(tc.tile_pool(name="lists", bufs=1))
+        keep = ctx.enter_context(tc.tile_pool(name="keep", bufs=1))
+        psum = ctx.enter_context(tc.psum_pool(name="psum", bufs=1))
+
+        def load_list(name, src):
+            tile = lists.tile(list(src.shape), U16, name=name)
+            nc.sync.dma_start(tile[:], src)
+            return tile
+
+        def load_words(name, src):
+            tile = keep.tile([P, src.shape[2]], U32, name=name, tag=name, align_bytes=64)
+            nc.sync.dma_start(tile[:].bitcast(I32), src[0].rearrange("p c r -> p (c r)").bitcast(I32))
+            return tile
+
+        def load_scale_rows(name, src):
+            tile = keep.tile([P, src.shape[2]], U8, name=name, align_bytes=64)
+            nc.vector.memset(tile[:].bitcast(I32), 0)
+            nc.scalar.dma_start(tile[:].bitcast(I32)[0:P:8, :], src[0].bitcast(I32))
+            return tile
+
+        def entries(tile, half):
+            cols = HALF // LIST_ROWS
+            return tile[:, half * cols : (half + 1) * cols]
+
+        d_scale_table = load_scale_rows("d_scale_table", d_scales)
+        x_scale_table = load_scale_rows("x_scale_table", x_scales)
+        k1_l = load_list("k1_l", k1)
+        offs_l = load_list("offs_l", offs)
+        d_word_table = load_words("d_word_table", d_words)
+        n2_l = load_list("n2_l", n2)
+        n1_l = load_list("n1_l", n1)
+        n3_l = load_list("n3_l", n3)
+        x_word_table = load_words("x_word_table", x_words)
+        n4_l = load_list("n4_l", n4)
+        n6_l = load_list("n6_l", n6)
+        n5_l = load_list("n5_l", n5)
+
+        d_bytes = keep.tile([P, H], U8, name="d_bytes", align_bytes=64)
+        x_bytes = keep.tile([P, S], U8, name="x_bytes", align_bytes=64)
+        scales1 = keep.tile([P, H + S], U8, name="scales1", align_bytes=64)
+        nc.vector.tensor_copy(d_bytes[:], d_scale_table[:].indirect(k1_l[:]))
+        nc.vector.tensor_copy(x_bytes[:], x_scale_table[:].indirect(offs_l[:]))
+        nc.vector.tensor_copy(
+            scales1[:, 0:H].rearrange("p (t c i) -> p c t i", t=PACK, i=16),
+            d_bytes[:].rearrange("p (c i t) -> p c t i", t=PACK, i=16),
+        )
+        nc.vector.tensor_copy(scales1[:, H : H + S], x_bytes[:])
+        scale_words = scales1[:].bitcast(I32)
+        for a in range(1, 4):
+            nc.scalar.dma_start(scale_words[a:P:32, :], scale_words[8 * a : P : 32, :])
+
+        d_picked = keep.tile([P, H], U32, name="d_picked", tag="d_picked", align_bytes=64)
+        d_dealt = keep.tile([P, H], U32, name="d_dealt", align_bytes=64)
+        x_picked = keep.tile([P, S], U32, name="x_picked", align_bytes=64)
+        nc.vector.tensor_copy(d_picked[:], d_word_table[:].indirect(k1_l[:]))
+        nc.vector.tensor_copy(
+            d_dealt[:].rearrange("p (t c i) -> p c t i", t=PACK, i=4),
+            d_picked[:].rearrange("p (c i t) -> p c t i", t=PACK, i=4),
+        )
+        nc.vector.tensor_copy(x_picked[:], x_word_table[:].indirect(offs_l[:]))
+
+        w_raw = keep.tile([P, PACK, N], F32, name="w_raw", tag="d_word_table", align_bytes=64)
+        nc.sync.dma_start(w_raw[:], w1.rearrange("(p t) n -> p t n", t=PACK))
+
+        gain = keep.tile([P, PACK], F32, name="gain", tag="d_picked", align_bytes=64)
+        nc.sync.dma_start(gain[:], gn.rearrange("(p t) o -> p (t o)", t=PACK))
+
+        h = []
+        for t in range(PACK):
+            cols = slice(t * P, (t + 1) * P)
+            acc = psum.tile([P, S], F32, name="acc_h%d" % t, tag="bank%d" % t)
+            nc.tensor.matmul_mx(
+                out=acc[:],
+                lhsT=d_dealt[:, cols].bitcast(FP8X4),
+                lhsT_scale=scales1[:, cols],
+                rhs=x_picked[:].bitcast(FP8X4),
+                rhs_scale=scales1[:, H : H + S],
+                start=True,
+                stop=True,
+            )
+            h_t = keep.tile([P, S], F32, name="h%d" % t)
+            nc.vector.tensor_scalar(h_t[:], acc[:], 0.0625, None, ALU.mult)
+            h.append(h_t)
+
+        dt = []
+        for t in range(PACK):
+            pairs = keep.tile([P, PACK, W], F32, name="pairs%d" % t, tag="pairs%d" % t)
+            pa, pb, rb = pairs[:, 0, :], pairs[:, 1, :], pairs[:, 2, :]
+            dt_t = keep.tile([P, S], F32, name="dt%d" % t)
+            nc.scalar.activation(pb, h[t][:].indirect(n2_l[:]), COPY)
+            nc.scalar.activation(pa, h[t][:].indirect(n1_l[:]), COPY)
+            nc.vector.tensor_tensor(rb, pa, pb, ALU.subtract)
+            nc.scalar.activation(dt_t[:].indirect(n1_l[:]), pb, COPY)
+            nc.scalar.activation(dt_t[:].indirect(n2_l[:]), rb, COPY)
+            dt.append(dt_t)
+
+        w_grouped = keep.tile([P, N, PACK], BF16, name="w_grouped", tag="grouped", align_bytes=64)
+        w_codes = keep.tile([P, N], U32, name="w_codes", align_bytes=64)
+        w_scales = keep.tile([P, N], U8, name="w_scales", align_bytes=64)
+        for u in range(N // P):
+            cols = slice(u * P, (u + 1) * P)
+            nc.vector.tensor_copy(
+                w_grouped[:, cols, :].rearrange("p (c i) t -> p c t i", i=4),
+                w_raw[:, :, cols].rearrange("p t (c i) -> p c t i", i=4),
+            )
+        for u in range(N // P):
+            cols = slice(u * P, (u + 1) * P)
+            nc.vector.quantize_mx(
+                out=w_codes[:, cols].bitcast(FP8X4),
+                scales=w_scales[:, cols],
+                in_=w_grouped[:, cols, :].rearrange("p n t -> p (n t)"),
+            )
+
+        z_codes = keep.tile([P, S], U32, name="z_codes", align_bytes=64)
+        z_scales = keep.tile([P, S], U8, name="z_scales", align_bytes=64)
+        h2 = [keep.tile([P, S], F32, name="h2_%d" % u) for u in range(N // P)]
+        page = [keep.tile([P, U], F32, name="page%d" % u) for u in range(N // P)]
+        for half in range(2):
+            js = slice(half * HALF, (half + 1) * HALF)
+            far = keep.tile([P, PACK, HALF], F32, name="far%d" % half, tag="pairs3" if half else "far0")
+            top = keep.tile([P, PACK, HALF], F32, name="top%d" % half, tag="top")
+            z = keep.tile([P, HALF, PACK], BF16, name="z%d" % half, tag="grouped", align_bytes=64)
+            for t in range(PACK):
+                nc.scalar.activation(far[:, t, :], dt[t][:].indirect(entries(n3_l, half)), COPY)
+                nc.vector.scalar_tensor_tensor(top[:, t, :], far[:, t, :], 0.5, dt[t][:, js], ALU.mult, ALU.max)
+                nc.vector.tensor_scalar(z[:, :, t], top[:, t, :], gain[:, t : t + 1], None, ALU.mult)
+            nc.vector.quantize_mx(
+                out=z_codes[:, js].bitcast(FP8X4),
+                scales=z_scales[:, js],
+                in_=z[:].rearrange("p j t -> p (j t)"),
+            )
+            for u in range(N // P):
+                cols = slice(u * P, (u + 1) * P)
+                acc = psum.tile([P, HALF], F32, name="acc_h2_%d_%d" % (half, u), tag="bank%d" % (u + PACK * (1 - half)))
+                nc.tensor.matmul_mx(
+                    out=acc[:],
+                    lhsT=w_codes[:, cols].bitcast(FP8X4),
+                    lhsT_scale=w_scales[:, cols],
+                    rhs=z_codes[:, js].bitcast(FP8X4),
+                    rhs_scale=z_scales[:, js],
+                    start=True,
+                    stop=True,
+                )
+                nc.vector.tensor_copy(h2[u][:, js], acc[:])
+
+        for u in range(N // P):
+            nc.scalar.activation(page[u][:].indirect(entries(n4_l, 0)), h2[u][:, 0:HALF], COPY)
+        for u in range(N // P):
+            other = keep.tile([P, S], F32, name="other%d" % u)
+            nw = keep.tile([P, S], F32, name="nw%d" % u)
+            for half in range(2):
+                js = slice(half * HALF, (half + 1) * HALF)
+                nc.scalar.activation(other[:, js], h2[u][:].indirect(entries(n6_l, half)), COPY)
+            nc.vector.tensor_tensor(nw[:], h2[u][:], other[:], ALU.subtract)
+            nc.scalar.activation(page[u][:].indirect(entries(n4_l, 1)), h2[u][:, HALF:S], COPY)
+            nc.scalar.activation(page[u][:].indirect(n5_l[:]), nw[:], COPY)
+            nc.sync.dma_start(out[u * P : (u + 1) * P, :], page[u][:])

@@ -41,28 +41,25 @@ def tile_picked_pqlayswapdpagq_none_p_kernel(tc, x_words, x_scales, d_words, d_s
         def load_scale_rows(name, src):
             tile = keep.tile([P, src.shape[2]], U8, name=name, align_bytes=64)
             nc.vector.memset(tile[:].bitcast(I32), 0)
-            nc.scalar.dma_start(tile[:].bitcast(I32)[0:P:8, :], src[0].bitcast(I32))
+            nc.sync.dma_start(tile[:].bitcast(I32)[0:P:8, :], src[0].bitcast(I32))
             return tile
 
         def entries(tile, half):
             cols = HALF // LIST_ROWS
             return tile[:, half * cols : (half + 1) * cols]
 
-        d_scale_table = load_scale_rows("d_scale_table", d_scales)
-        x_scale_table = load_scale_rows("x_scale_table", x_scales)
         k1_l = load_list("k1_l", k1)
         offs_l = load_list("offs_l", offs)
+        d_scale_table = load_scale_rows("d_scale_table", d_scales)
+        x_scale_table = load_scale_rows("x_scale_table", x_scales)
         d_word_table = load_words("d_word_table", d_words)
         n2_l = load_list("n2_l", n2)
         n1_l = load_list("n1_l", n1)
-        n3_l = load_list("n3_l", n3)
         x_word_table = load_words("x_word_table", x_words)
-        n4_l = load_list("n4_l", n4)
-        n6_l = load_list("n6_l", n6)
-        n5_l = load_list("n5_l", n5)
+        n3_l = load_list("n3_l", n3)
 
         d_bytes = keep.tile([P, H], U8, name="d_bytes", align_bytes=64)
-        x_bytes = keep.tile([P, S], U8, name="x_bytes", align_bytes=64)
+        x_bytes = keep.tile([P, S], U8, name="x_bytes", tag="d_picked", align_bytes=64)
         scales1 = keep.tile([P, H + S], U8, name="scales1", align_bytes=64)
         nc.vector.tensor_copy(d_bytes[:], d_scale_table[:].indirect(k1_l[:]))
         nc.vector.tensor_copy(x_bytes[:], x_scale_table[:].indirect(offs_l[:]))
@@ -70,7 +67,7 @@ def tile_picked_pqlayswapdpagq_none_p_kernel(tc, x_words, x_scales, d_words, d_s
             scales1[:, 0:H].rearrange("p (t c i) -> p c t i", t=PACK, i=16),
             d_bytes[:].rearrange("p (c i t) -> p c t i", t=PACK, i=16),
         )
-        nc.vector.tensor_copy(scales1[:, H : H + S], x_bytes[:])
+        nc.vector.tensor_copy(scales1[:, H : H + S].bitcast(I32), x_bytes[:].bitcast(I32))
         scale_words = scales1[:].bitcast(I32)
         for a in range(1, 4):
             nc.scalar.dma_start(scale_words[a:P:32, :], scale_words[8 * a : P : 32, :])
@@ -83,7 +80,9 @@ def tile_picked_pqlayswapdpagq_none_p_kernel(tc, x_words, x_scales, d_words, d_s
             d_dealt[:].rearrange("p (t c i) -> p c t i", t=PACK, i=4),
             d_picked[:].rearrange("p (c i t) -> p c t i", t=PACK, i=4),
         )
-        nc.vector.tensor_copy(x_picked[:], x_word_table[:].indirect(offs_l[:]))
+        for half in range(2):
+            js = slice(half * HALF, (half + 1) * HALF)
+            nc.vector.tensor_copy(x_picked[:, js], x_word_table[:].indirect(entries(offs_l, half)))
 
         w_raw = keep.tile([P, PACK, N], F32, name="w_raw", tag="d_word_table", align_bytes=64)
         nc.sync.dma_start(w_raw[:], w1.rearrange("(p t) n -> p t n", t=PACK))
@@ -91,30 +90,36 @@ def tile_picked_pqlayswapdpagq_none_p_kernel(tc, x_words, x_scales, d_words, d_s
         gain = keep.tile([P, PACK], F32, name="gain", tag="d_picked", align_bytes=64)
         nc.sync.dma_start(gain[:], gn.rearrange("(p t) o -> p (t o)", t=PACK))
 
-        h = []
+        n4_l = load_list("n4_l", n4)
+        n6_l = load_list("n6_l", n6)
+        n5_l = load_list("n5_l", n5)
+
+        rows = [keep.tile([P, 2 * S], F32, name="rows%d" % t) for t in range(PACK)]
+        h2 = [rows[t][:, 0:S] for t in range(PACK)]
+        h = [rows[t][:, S : 2 * S] for t in range(PACK)]
         for t in range(PACK):
             cols = slice(t * P, (t + 1) * P)
-            acc = psum.tile([P, S], F32, name="acc_h%d" % t, tag="bank%d" % t)
-            nc.tensor.matmul_mx(
-                out=acc[:],
-                lhsT=d_dealt[:, cols].bitcast(FP8X4),
-                lhsT_scale=scales1[:, cols],
-                rhs=x_picked[:].bitcast(FP8X4),
-                rhs_scale=scales1[:, H : H + S],
-                start=True,
-                stop=True,
-            )
-            h_t = keep.tile([P, S], F32, name="h%d" % t)
-            nc.vector.tensor_scalar(h_t[:], acc[:], 0.0625, None, ALU.mult)
-            h.append(h_t)
+            width = HALF if t == 0 else S
+            for j0 in range(0, S, width):
+                acc = psum.tile([P, width], F32, name="acc_h%d_%d" % (t, j0), tag="bank%d" % (t + PACK * (j0 // width)))
+                nc.tensor.matmul_mx(
+                    out=acc[:],
+                    lhsT=d_dealt[:, cols].bitcast(FP8X4),
+                    lhsT_scale=scales1[:, cols],
+                    rhs=x_picked[:, j0 : j0 + width].bitcast(FP8X4),
+                    rhs_scale=scales1[:, H + j0 : H + j0 + width],
+                    start=True,
+                    stop=True,
+                )
+                nc.vector.tensor_scalar(h[t][:, j0 : j0 + width], acc[:], 0.0625, None, ALU.mult)
 
         dt = []
         for t in range(PACK):
             pairs = keep.tile([P, PACK, W], F32, name="pairs%d" % t, tag="pairs%d" % t)
             pa, pb, rb = pairs[:, 0, :], pairs[:, 1, :], pairs[:, 2, :]
             dt_t = keep.tile([P, S], F32, name="dt%d" % t)
-            nc.scalar.activation(pb, h[t][:].indirect(n2_l[:]), COPY)
-            nc.scalar.activation(pa, h[t][:].indirect(n1_l[:]), COPY)
+            nc.scalar.activation(pb, h[t].indirect(n2_l[:]), COPY)
+            nc.scalar.activation(pa, h[t].indirect(n1_l[:]), COPY)
             nc.vector.tensor_tensor(rb, pa, pb, ALU.subtract)
             nc.scalar.activation(dt_t[:].indirect(n1_l[:]), pb, COPY)
             nc.scalar.activation(dt_t[:].indirect(n2_l[:]), rb, COPY)
@@ -139,7 +144,6 @@ def tile_picked_pqlayswapdpagq_none_p_kernel(tc, x_words, x_scales, d_words, d_s
 
         z_codes = keep.tile([P, S], U32, name="z_codes", align_bytes=64)
         z_scales = keep.tile([P, S], U8, name="z_scales", align_bytes=64)
-        h2 = [keep.tile([P, S], F32, name="h2_%d" % u) for u in range(N // P)]
         page = [keep.tile([P, U], F32, name="page%d" % u) for u in range(N // P)]
         for half in range(2):
             js = slice(half * HALF, (half + 1) * HALF)
@@ -174,10 +178,8 @@ def tile_picked_pqlayswapdpagq_none_p_kernel(tc, x_words, x_scales, d_words, d_s
         for u in range(N // P):
             other = keep.tile([P, S], F32, name="other%d" % u)
             nw = keep.tile([P, S], F32, name="nw%d" % u)
-            for half in range(2):
-                js = slice(half * HALF, (half + 1) * HALF)
-                nc.scalar.activation(other[:, js], h2[u][:].indirect(entries(n6_l, half)), COPY)
-            nc.vector.tensor_tensor(nw[:], h2[u][:], other[:], ALU.subtract)
+            nc.scalar.activation(other[:], rows[u][:].indirect(n6_l[:]), COPY)
+            nc.vector.tensor_tensor(nw[:], h2[u], other[:], ALU.subtract)
             nc.scalar.activation(page[u][:].indirect(entries(n4_l, 1)), h2[u][:, HALF:S], COPY)
             nc.scalar.activation(page[u][:].indirect(n5_l[:]), nw[:], COPY)
             nc.sync.dma_start(out[u * P : (u + 1) * P, :], page[u][:])

@@ -19,6 +19,7 @@ P = 128
 PACK = 4
 HALF = S // 2
 LIST_ROWS = 16
+PIECES = (slice(0, 64), slice(64, 128), slice(128, 256))
 
 
 def tile_picked_pqlayswapdpagq_none_p_kernel(tc, x_words, x_scales, d_words, d_scales, gn, w1, offs, k1, n1, n2, n3, n4, n5, n6, out):
@@ -44,17 +45,16 @@ def tile_picked_pqlayswapdpagq_none_p_kernel(tc, x_words, x_scales, d_words, d_s
             nc.sync.dma_start(tile[:].bitcast(I32)[0:P:8, :], src[0].bitcast(I32))
             return tile
 
-        def entries(tile, half):
-            cols = HALF // LIST_ROWS
-            return tile[:, half * cols : (half + 1) * cols]
+        def entries(tile, js):
+            return tile[:, js.start // LIST_ROWS : js.stop // LIST_ROWS]
 
         k1_l = load_list("k1_l", k1)
         offs_l = load_list("offs_l", offs)
+        n2_l = load_list("n2_l", n2)
+        n1_l = load_list("n1_l", n1)
         d_scale_table = load_scale_rows("d_scale_table", d_scales)
         x_scale_table = load_scale_rows("x_scale_table", x_scales)
         d_word_table = load_words("d_word_table", d_words)
-        n2_l = load_list("n2_l", n2)
-        n1_l = load_list("n1_l", n1)
         x_word_table = load_words("x_word_table", x_words)
         n3_l = load_list("n3_l", n3)
 
@@ -82,7 +82,7 @@ def tile_picked_pqlayswapdpagq_none_p_kernel(tc, x_words, x_scales, d_words, d_s
         )
         for half in range(2):
             js = slice(half * HALF, (half + 1) * HALF)
-            nc.vector.tensor_copy(x_picked[:, js], x_word_table[:].indirect(entries(offs_l, half)))
+            nc.vector.tensor_copy(x_picked[:, js], x_word_table[:].indirect(entries(offs_l, js)))
 
         w_raw = keep.tile([P, PACK, N], F32, name="w_raw", tag="d_word_table", align_bytes=64)
         nc.sync.dma_start(w_raw[:], w1.rearrange("(p t) n -> p t n", t=PACK))
@@ -145,13 +145,15 @@ def tile_picked_pqlayswapdpagq_none_p_kernel(tc, x_words, x_scales, d_words, d_s
         z_codes = keep.tile([P, S], U32, name="z_codes", align_bytes=64)
         z_scales = keep.tile([P, S], U8, name="z_scales", align_bytes=64)
         page = [keep.tile([P, U], F32, name="page%d" % u) for u in range(N // P)]
-        for half in range(2):
-            js = slice(half * HALF, (half + 1) * HALF)
-            far = keep.tile([P, PACK, HALF], F32, name="far%d" % half, tag="pairs3" if half else "far0")
-            top = keep.tile([P, PACK, HALF], F32, name="top%d" % half, tag="top")
-            z = keep.tile([P, HALF, PACK], BF16, name="z%d" % half, tag="grouped", align_bytes=64)
+        far_first = keep.tile([P, PACK, PIECES[0].stop], F32, name="far_first")
+        far_rest = keep.tile([P, PACK, S - PIECES[0].stop], F32, name="far_rest", tag="pairs3")
+        for piece, js in enumerate(PIECES):
+            width = js.stop - js.start
+            far = far_rest[:, :, js.start - PIECES[0].stop : js.stop - PIECES[0].stop] if piece else far_first[:]
+            top = keep.tile([P, PACK, width], F32, name="top%d" % piece, tag="grouped" if piece == 2 else "top", align_bytes=64)
+            z = keep.tile([P, width, PACK], BF16, name="z%d" % piece, tag="z%d" % piece if piece else "grouped", align_bytes=64)
             for t in range(PACK):
-                nc.scalar.activation(far[:, t, :], dt[t][:].indirect(entries(n3_l, half)), COPY)
+                nc.scalar.activation(far[:, t, :], dt[t][:].indirect(entries(n3_l, js)), COPY)
                 nc.vector.scalar_tensor_tensor(top[:, t, :], far[:, t, :], 0.5, dt[t][:, js], ALU.mult, ALU.max)
                 nc.vector.tensor_scalar(z[:, :, t], top[:, t, :], gain[:, t : t + 1], None, ALU.mult)
             nc.vector.quantize_mx(
@@ -161,7 +163,7 @@ def tile_picked_pqlayswapdpagq_none_p_kernel(tc, x_words, x_scales, d_words, d_s
             )
             for u in range(N // P):
                 cols = slice(u * P, (u + 1) * P)
-                acc = psum.tile([P, HALF], F32, name="acc_h2_%d_%d" % (half, u), tag="bank%d" % (u + PACK * (1 - half)))
+                acc = psum.tile([P, width], F32, name="acc_h2_%d_%d" % (piece, u), tag="bank%d" % (u + PACK * ((piece + 1) % 2)))
                 nc.tensor.matmul_mx(
                     out=acc[:],
                     lhsT=w_codes[:, cols].bitcast(FP8X4),
@@ -173,13 +175,14 @@ def tile_picked_pqlayswapdpagq_none_p_kernel(tc, x_words, x_scales, d_words, d_s
                 )
                 nc.vector.tensor_copy(h2[u][:, js], acc[:])
 
-        for u in range(N // P):
-            nc.scalar.activation(page[u][:].indirect(entries(n4_l, 0)), h2[u][:, 0:HALF], COPY)
+        for js in PIECES[:-1]:
+            for u in range(N // P):
+                nc.scalar.activation(page[u][:].indirect(entries(n4_l, js)), h2[u][:, js], COPY)
         for u in range(N // P):
             other = keep.tile([P, S], F32, name="other%d" % u)
             nw = keep.tile([P, S], F32, name="nw%d" % u)
             nc.scalar.activation(other[:], rows[u][:].indirect(n6_l[:]), COPY)
             nc.vector.tensor_tensor(nw[:], h2[u], other[:], ALU.subtract)
-            nc.scalar.activation(page[u][:].indirect(entries(n4_l, 1)), h2[u][:, HALF:S], COPY)
+            nc.scalar.activation(page[u][:].indirect(entries(n4_l, PIECES[-1])), h2[u][:, PIECES[-1]], COPY)
             nc.scalar.activation(page[u][:].indirect(n5_l[:]), nw[:], COPY)
             nc.sync.dma_start(out[u * P : (u + 1) * P, :], page[u][:])

from contextlib import ExitStack

import concourse.mybir as mybir

K, T, S, N, G, H, W, U = 512, 2048, 256, 512, 2048, 512, 128, 512
FLOPS = 2 * K * H * S + 2 * H * N * S

F32 = mybir.dt.float32
BF16 = mybir.dt.bfloat16
I32 = mybir.dt.int32
U32 = mybir.dt.uint32
U16 = mybir.dt.uint16
U8 = mybir.dt.uint8
FP8X4 = mybir.dt.float8_e4m3fn_x4
ALU = mybir.AluOpType
COPY = mybir.ActivationFunctionType.Copy

P = 128
PACK = 4
HALF = S // 2
LIST_ROWS = 16
PIECES = (slice(0, 64), slice(64, 128), slice(128, 256))


def tile_picked_pqlayswapdpagq_none_p_kernel(tc, x_words, x_scales, d_words, d_scales, gn, w1, offs, k1, n1, n2, n3, n4, n5, n6, out):
    nc = tc.nc
    with ExitStack() as ctx:
        lists = ctx.enter_context(tc.tile_pool(name="lists", bufs=1))
        keep = ctx.enter_context(tc.tile_pool(name="keep", bufs=1))
        psum = ctx.enter_context(tc.psum_pool(name="psum", bufs=1))

        def load_list(name, src):
            tile = lists.tile(list(src.shape), U16, name=name)
            nc.sync.dma_start(tile[:], src)
            return tile

        def load_words(name, src):
            tile = keep.tile([P, src.shape[2]], U32, name=name, tag=name, align_bytes=64)
            nc.sync.dma_start(tile[:].bitcast(I32), src[0].rearrange("p c r -> p (c r)").bitcast(I32))
            return tile

        def load_scale_rows(name, src):
            tile = keep.tile([P, src.shape[2]], U8, name=name, align_bytes=64)
            nc.vector.memset(tile[:].bitcast(I32), 0)
            nc.sync.dma_start(tile[:].bitcast(I32)[0:P:8, :], src[0].bitcast(I32))
            return tile

        def entries(tile, js):
            return tile[:, js.start // LIST_ROWS : js.stop // LIST_ROWS]

        k1_l = load_list("k1_l", k1)
        offs_l = load_list("offs_l", offs)
        n2_l = load_list("n2_l", n2)
        n1_l = load_list("n1_l", n1)
        d_scale_table = load_scale_rows("d_scale_table", d_scales)
        x_scale_table = load_scale_rows("x_scale_table", x_scales)
        d_word_table = load_words("d_word_table", d_words)
        x_word_table = load_words("x_word_table", x_words)
        n3_l = load_list("n3_l", n3)

        d_bytes = keep.tile([P, H], U8, name="d_bytes", align_bytes=64)
        x_bytes = keep.tile([P, S], U8, name="x_bytes", tag="d_picked", align_bytes=64)
        scales1 = keep.tile([P, H + S], U8, name="scales1", align_bytes=64)
        nc.vector.tensor_copy(d_bytes[:], d_scale_table[:].indirect(k1_l[:]))
        nc.vector.tensor_copy(x_bytes[:], x_scale_table[:].indirect(offs_l[:]))
        nc.vector.tensor_copy(
            scales1[:, 0:H].rearrange("p (t c i) -> p c t i", t=PACK, i=16),
            d_bytes[:].rearrange("p (c i t) -> p c t i", t=PACK, i=16),
        )
        nc.vector.tensor_copy(scales1[:, H : H + S].bitcast(I32), x_bytes[:].bitcast(I32))
        scale_words = scales1[:].bitcast(I32)
        for a in range(1, 4):
            nc.scalar.dma_start(scale_words[a:P:32, :], scale_words[8 * a : P : 32, :])

        d_picked = keep.tile([P, H], U32, name="d_picked", tag="d_picked", align_bytes=64)
        d_dealt = keep.tile([P, H], U32, name="d_dealt", align_bytes=64)
        x_picked = keep.tile([P, S], U32, name="x_picked", align_bytes=64)
        nc.vector.tensor_copy(d_picked[:], d_word_table[:].indirect(k1_l[:]))
        nc.vector.tensor_copy(
            d_dealt[:].rearrange("p (t c i) -> p c t i", t=PACK, i=4),
            d_picked[:].rearrange("p (c i t) -> p c t i", t=PACK, i=4),
        )
        for half in range(2):
            js = slice(half * HALF, (half + 1) * HALF)
            nc.vector.tensor_copy(x_picked[:, js], x_word_table[:].indirect(entries(offs_l, js)))

        w_raw = keep.tile([P, PACK, N], F32, name="w_raw", tag="d_word_table", align_bytes=64)
        nc.sync.dma_start(w_raw[:], w1.rearrange("(p t) n -> p t n", t=PACK))

        gain = keep.tile([P, PACK], F32, name="gain", tag="d_picked", align_bytes=64)
        nc.sync.dma_start(gain[:], gn.rearrange("(p t) o -> p (t o)", t=PACK))

        n4_l = load_list("n4_l", n4)
        n6_l = load_list("n6_l", n6)
        n5_l = load_list("n5_l", n5)

        rows = [keep.tile([P, 2 * S], F32, name="rows%d" % t) for t in range(PACK)]
        h2 = [rows[t][:, 0:S] for t in range(PACK)]
        h = [rows[t][:, S : 2 * S] for t in range(PACK)]
        for t in range(PACK):
            cols = slice(t * P, (t + 1) * P)
            width = HALF if t == 0 else S
            for j0 in range(0, S, width):
                acc = psum.tile([P, width], F32, name="acc_h%d_%d" % (t, j0), tag="bank%d" % (t + PACK * (j0 // width)))
                nc.tensor.matmul_mx(
                    out=acc[:],
                    lhsT=d_dealt[:, cols].bitcast(FP8X4),
                    lhsT_scale=scales1[:, cols],
                    rhs=x_picked[:, j0 : j0 + width].bitcast(FP8X4),
                    rhs_scale=scales1[:, H + j0 : H + j0 + width],
                    start=True,
                    stop=True,
                )
                nc.vector.tensor_scalar(h[t][:, j0 : j0 + width], acc[:], 0.0625, None, ALU.mult)

        dt = []
        for t in range(PACK):
            pairs = keep.tile([P, PACK, W], F32, name="pairs%d" % t, tag="pairs%d" % t)
            pa, pb, rb = pairs[:, 0, :], pairs[:, 1, :], pairs[:, 2, :]
            dt_t = keep.tile([P, S], F32, name="dt%d" % t)
            nc.scalar.activation(pb, h[t].indirect(n2_l[:]), COPY)
            nc.scalar.activation(pa, h[t].indirect(n1_l[:]), COPY)
            nc.vector.tensor_tensor(rb, pa, pb, ALU.subtract)
            nc.scalar.activation(dt_t[:].indirect(n1_l[:]), pb, COPY)
            nc.scalar.activation(dt_t[:].indirect(n2_l[:]), rb, COPY)
            dt.append(dt_t)

        w_grouped = keep.tile([P, N, PACK], BF16, name="w_grouped", tag="grouped", align_bytes=64)
        w_codes = keep.tile([P, N], U32, name="w_codes", align_bytes=64)
        w_scales = keep.tile([P, N], U8, name="w_scales", align_bytes=64)
        for u in range(N // P):
            cols = slice(u * P, (u + 1) * P)
            nc.vector.tensor_copy(
                w_grouped[:, cols, :].rearrange("p (c i) t -> p c t i", i=4),
                w_raw[:, :, cols].rearrange("p t (c i) -> p c t i", i=4),
            )
        for u in range(N // P):
            cols = slice(u * P, (u + 1) * P)
            nc.vector.quantize_mx(
                out=w_codes[:, cols].bitcast(FP8X4),
                scales=w_scales[:, cols],
                in_=w_grouped[:, cols, :].rearrange("p n t -> p (n t)"),
            )

        z_codes = keep.tile([P, S], U32, name="z_codes", align_bytes=64)
        z_scales = keep.tile([P, S], U8, name="z_scales", align_bytes=64)
        page = [keep.tile([P, U], F32, name="page%d" % u) for u in range(N // P)]
        far_first = keep.tile([P, PACK, PIECES[0].stop], F32, name="far_first")
        far_rest = keep.tile([P, PACK, S - PIECES[0].stop], F32, name="far_rest", tag="pairs3")
        for piece, js in enumerate(PIECES):
            width = js.stop - js.start
            far = far_rest[:, :, js.start - PIECES[0].stop : js.stop - PIECES[0].stop] if piece else far_first[:]
            top = keep.tile([P, PACK, width], F32, name="top%d" % piece, tag="grouped" if piece == 2 else "top", align_bytes=64)
            z = keep.tile([P, width, PACK], BF16, name="z%d" % piece, tag="z%d" % piece if piece else "grouped", align_bytes=64)
            for t in range(PACK):
                nc.scalar.activation(far[:, t, :], dt[t][:].indirect(entries(n3_l, js)), COPY)
                nc.vector.scalar_tensor_tensor(top[:, t, :], far[:, t, :], 0.5, dt[t][:, js], ALU.mult, ALU.max)
                nc.vector.tensor_scalar(z[:, :, t], top[:, t, :], gain[:, t : t + 1], None, ALU.mult)
            nc.vector.quantize_mx(
                out=z_codes[:, js].bitcast(FP8X4),
                scales=z_scales[:, js],
                in_=z[:].rearrange("p j t -> p (j t)"),
            )
            for u in range(N // P):
                cols = slice(u * P, (u + 1) * P)
                acc = psum.tile([P, width], F32, name="acc_h2_%d_%d" % (piece, u), tag="bank%d" % (u + PACK * ((piece + 1) % 2)))
                nc.tensor.matmul_mx(
                    out=acc[:],
                    lhsT=w_codes[:, cols].bitcast(FP8X4),
                    lhsT_scale=w_scales[:, cols],
                    rhs=z_codes[:, js].bitcast(FP8X4),
                    rhs_scale=z_scales[:, js],
                    start=True,
                    stop=True,
                )
                nc.vector.tensor_copy(h2[u][:, js], acc[:])

        for js in PIECES[:-1]:
            for u in range(N // P):
                nc.scalar.activation(page[u][:].indirect(entries(n4_l, js)), h2[u][:, js], COPY)
        for u in range(N // P):
            other = keep.tile([P, S], F32, name="other%d" % u)
            nw = keep.tile([P, S], F32, name="nw%d" % u)
            nc.scalar.activation(other[:], rows[u][:].indirect(n6_l[:]), COPY)
            nc.vector.tensor_tensor(nw[:], h2[u], other[:], ALU.subtract)
            nc.scalar.activation(page[u][:].indirect(entries(n4_l, PIECES[-1])), h2[u][:, PIECES[-1]], COPY)
            nc.scalar.activation(page[u][:].indirect(n5_l[:]), nw[:], COPY)
            nc.sync.dma_start(out[u * P : (u + 1) * P, :], page[u][:])
